import numpy as np
import ml_dtypes


def mxq(x, axis, fmt="e4m3"):
    dtype, down = {"e4m3": (ml_dtypes.float8_e4m3fn, 7), "e5m2": (ml_dtypes.float8_e5m2, 14)}[fmt]
    v = np.moveaxis(np.asarray(x, np.float32).astype(ml_dtypes.bfloat16).astype(np.float64), axis, -1)
    blocks = v.reshape(v.shape[:-1] + (-1, 32))
    amax = np.abs(blocks).max(-1, keepdims=True)
    byte = np.maximum(np.where(amax > 0, np.frexp(amax)[1] - 1 + 127, 0) - down, 1)
    scale = np.exp2(byte - 127.0)
    codes = (blocks / scale).astype(np.float32).astype(dtype).astype(np.float64)
    return np.moveaxis((codes * scale).reshape(v.shape), -1, axis)


WIDE = False


def mx_kscale(k):
    if not WIDE:
        return np.ones(k)
    levels = np.array([10, -10, 5, -5, 0])
    if k % 512:
        return np.exp2(np.random.permutation(np.resize(levels, k // 32))).repeat(32)
    a = np.empty((k // 512, 16))
    for p in range(k // 512):
        a[p, :8] = np.random.permutation(np.resize(levels, 8))
        for g in range(8):
            far = levels[np.abs(levels - a[p, g]) >= 10]
            a[p, g + 8] = far[np.random.randint(len(far))]
    return np.exp2(a.ravel()).repeat(32)


def f64(x):
    return np.asarray(x).astype(np.float64)


def striped(idx):
    return np.tile(idx.reshape(-1, 16).T, (8, 1)).astype(np.uint16)


def unstriped(offs):
    return offs[:16].T.reshape(-1).astype(np.int64)


E2M1 = np.array([0.0, 0.5, 1.0, 1.5, 2.0, 3.0, 4.0, 6.0, -0.0, -0.5, -1.0, -1.5, -2.0, -3.0, -4.0, -6.0])


def pack_fp4(w):
    k, n = w.shape
    w = f64(np.asarray(w, np.float32).astype(ml_dtypes.bfloat16)).reshape(k // 32, 32, n)
    amax = np.abs(w).max(1)
    mant, ex = np.frexp(amax / 6.0)
    byte = np.clip(np.where(amax > 0, np.where(mant > 0.5, ex, ex - 1) + 127, 1), 1, 254)
    scaled = (w * np.exp2(127.0 - byte)[:, None, :]).reshape(k, n).astype(np.float32)
    c = np.ascontiguousarray(scaled.reshape(k // 512, 128, 4, n).transpose(0, 1, 3, 2)).astype(ml_dtypes.float4_e2m1fn).view(np.uint8) & 0xF
    words = (c[..., 0::2] | (c[..., 1::2] << 4)).reshape(k // 512, 128, 2 * n)
    return np.ascontiguousarray(words), np.ascontiguousarray(byte.astype(np.uint8).reshape(k // 512, 16, n))


def unpack_fp4(words, scales):
    g, _, n = scales.shape
    words = np.ascontiguousarray(words).reshape(g, 128, n, 2)
    nib = np.empty((g, 128, n, 4), np.uint8)
    nib[..., 0::2] = words & 0xF
    nib[..., 1::2] = words >> 4
    vals = E2M1[nib] * np.repeat(np.exp2(scales.astype(np.float64) - 127.0), 8, axis=1)[..., None]
    return vals.transpose(0, 1, 3, 2).reshape(g * 512, n)


K, T, S, V, N = 512, 4096, 1024, 512, 256


def setup_inputs():
    n = np.random.standard_normal
    s = mx_kscale(K)[:, None]
    packed_w1 = pack_fp4(n((K, N)) / np.sqrt(K) / s)
    packed_w2 = pack_fp4(n((K, N)) / np.sqrt(K) / s)
    return {
        "xT": (n((K, T)) * s).astype(np.float32),
        "sT": (n((K, V)) * s).astype(np.float32),
        "w1_words": packed_w1[0],
        "w1_scales": packed_w1[1],
        "w2_words": packed_w2[0],
        "w2_scales": packed_w2[1],
        "offs": striped(np.random.permutation(T)[:S]),
        "par": striped(np.random.randint(0, V, S)),
    }


def reference(xT, sT, w1_words, w1_scales, w2_words, w2_scales, offs, par):
    xq = mxq(f64(xT)[:, unstriped(offs)], 0, "e4m3")
    y = unpack_fp4(w1_words, w1_scales).T @ xq
    t = unpack_fp4(w2_words, w2_scales).T @ mxq(f64(sT), 0, "e4m3")
    return y + t[:, unstriped(par)]

@@ -1,0 +1,164 @@
+from contextlib import ExitStack
+
+import concourse.mybir as mybir
+
+K, T, S, V, N = 512, 4096, 1024, 512, 256
+FLOPS = 2 * K * N * (S + V)
+
+F32 = mybir.dt.float32
+BF16 = mybir.dt.bfloat16
+I32 = mybir.dt.int32
+U32 = mybir.dt.uint32
+U16 = mybir.dt.uint16
+U8 = mybir.dt.uint8
+FP8X4 = mybir.dt.float8_e4m3fn_x4
+FP4X4 = mybir.dt.float4_e2m1fn_x4
+COPY = mybir.ActivationFunctionType.Copy
+ADD = mybir.AluOpType.add
+
+P = 128
+PACK = 4
+HALF = S // 2
+PAR_PIECE = 256
+LAST_CHUNKS = ((1024, "scalar"), (1024, "scalar"), (768, "scalar"), (512, "vector"), (512, "vector"), (256, "scalar"))
+
+
+def tile_picked_fpn_none_e_kernel(
+    tc, xT, sT, w1_words, w1_scales, w2_words, w2_scales, offs, par, out
+):
+    nc = tc.nc
+    with ExitStack() as ctx:
+        keep = ctx.enter_context(tc.tile_pool(name="keep", bufs=1))
+        psum = ctx.enter_context(tc.psum_pool(name="psum", bufs=1))
+
+        offs_sb = keep.tile([P, S // 16], U16, name="offs_sb")
+        par_sb = keep.tile([P, S // 16], U16, name="par_sb")
+
+        def entries(list_sb, first, count):
+            return list_sb[:, first // 16 : (first + count) // 16]
+
+        w2_plane = keep.tile([P, N], U8, name="w2_plane", align_bytes=64)
+        w1_plane = keep.tile([P, N], U8, name="w1_plane", align_bytes=64)
+        for plane in (w2_plane, w1_plane):
+            nc.vector.memset(plane[:].bitcast(I32), 0)
+
+        def load_scales(plane, scales):
+            for q in range(4):
+                nc.sync.dma_start(
+                    out=plane[32 * q : 32 * q + 4, :].bitcast(I32),
+                    in_=scales[0, 4 * q : 4 * q + 4, :].bitcast(I32),
+                )
+
+        s_raw = keep.tile([P, PACK, V], F32, name="s_raw")
+        w2_sb = keep.tile([P, 2 * N], U8, name="w2_sb", align_bytes=64)
+        w1_sb = keep.tile([P, 2 * N], U8, name="w1_sb", align_bytes=64)
+        x_rows = [keep.tile([P, T], F32, name=f"x_row{t}", tag=f"x_row{t}") for t in range(PACK)]
+        x_view = xT.rearrange("(p t) c -> p t c", t=PACK)
+
+        nc.sync.dma_start(out=s_raw[:], in_=sT.rearrange("(p t) v -> p t v", t=PACK))
+        nc.sync.dma_start(out=w2_sb[:].bitcast(I32), in_=w2_words[0].bitcast(I32))
+        nc.sync.dma_start(par_sb[:], par)
+        load_scales(w2_plane, w2_scales)
+        nc.sync.dma_start(out=x_rows[0][:], in_=x_view[:, 0, :])
+        nc.sync.dma_start(offs_sb[:], offs)
+        nc.sync.dma_start(out=w1_sb[:].bitcast(I32), in_=w1_words[0].bitcast(I32))
+        nc.sync.dma_start(out=x_rows[1][:], in_=x_view[:, 1, :])
+        load_scales(w1_plane, w1_scales)
+        nc.sync.dma_start(out=x_rows[2][:], in_=x_view[:, 2, :])
+        chunks = []
+        first = 0
+        for width, engine in LAST_CHUNKS:
+            cols = slice(first, first + width)
+            nc.sync.dma_start(out=x_rows[3][:, cols], in_=x_view[:, 3, cols])
+            chunks.append((cols, engine))
+            first = first + width
+
+        def quantize(name, grouped, width):
+            codes = keep.tile([P, width], U32, name=name + "_codes", align_bytes=64)
+            scales = keep.tile([P, width], U8, name=name + "_scales", align_bytes=64)
+            nc.vector.quantize_mx(
+                out=codes[:].bitcast(FP8X4), scales=scales[:], in_=grouped.rearrange("p c t -> p (c t)")
+            )
+            return codes, scales
+
+        def product(acc, w_sb, w_plane, h, codes, scales):
+            nc.tensor.matmul_mx(
+                out=acc,
+                lhsT=w_sb[:, 2 * P * h : 2 * P * (h + 1)].bitcast(FP4X4),
+                lhsT_scale=w_plane[:, P * h : P * (h + 1)],
+                rhs=codes[:].bitcast(FP8X4),
+                rhs_scale=scales[:],
+                start=True,
+                stop=True,
+            )
+
+        s_quantised = []
+        for b in range(2):
+            cells = s_raw[:, :, V // 2 * b : V // 2 * (b + 1)].rearrange("p t v -> p v t")
+            s_grouped = keep.tile([P, V // 2, PACK], BF16, name=f"s_grouped{b}", align_bytes=64)
+            if b == 0:
+                nc.vector.tensor_copy(out=s_grouped[:], in_=cells)
+            else:
+                nc.scalar.activation(s_grouped[:], cells, COPY)
+            s_quantised.append(quantize(f"s{b}", s_grouped[:], V // 2))
+        t_sbs = []
+        for h in range(N // P):
+            t_acc = psum.tile([P, V], F32, name=f"t_acc{h}")
+            for b in range(2):
+                product(t_acc[:, V // 2 * b : V // 2 * (b + 1)], w2_sb, w2_plane, h, *s_quantised[b])
+            t_sb = keep.tile([P, V], F32, name=f"t_sb{h}")
+            nc.scalar.activation(t_sb[:], t_acc[:], COPY)
+            t_sbs.append(t_sb)
+
+        parents = {}
+
+        def fetch_parents(b, h, tag):
+            parent = keep.tile([P, HALF], F32, name=f"parent{b}{h}", tag=tag)
+            for first in range(0, HALF, PAR_PIECE):
+                nc.vector.tensor_copy(
+                    parent[:, first : first + PAR_PIECE],
+                    t_sbs[h][:].indirect(entries(par_sb, HALF * b + first, PAR_PIECE)),
+                )
+            parents[b, h] = parent
+
+        for b, h in ((0, 0), (1, 0), (0, 1)):
+            fetch_parents(b, h, f"parent{b}{h}")
+
+        grouped = [keep.tile([P, HALF, PACK], BF16, name=f"grouped{b}", align_bytes=64) for b in range(2)]
+        picked01 = keep.tile([P, 2, S], BF16, name="picked01")
+        for t in range(2):
+            nc.vector.tensor_copy(picked01[:, t, :], x_rows[t][:].indirect(offs_sb[:]))
+        fetch_parents(1, 1, "x_row1")
+        for b in range(2):
+            nc.scalar.activation(
+                grouped[b][:, :, 0:2],
+                picked01[:, :, HALF * b : HALF * (b + 1)].rearrange("p t c -> p c t"),
+                COPY,
+            )
+        for b in (1, 0):
+            nc.vector.tensor_copy(grouped[b][:, :, 2], x_rows[2][:].indirect(entries(offs_sb, HALF * b, HALF)))
+
+        x3_bf16 = keep.tile([P, T], BF16, name="x3_bf16")
+        for cols, engine in chunks:
+            if engine == "scalar":
+                nc.scalar.activation(x3_bf16[:, cols], x_rows[3][:, cols], COPY)
+            else:
+                nc.vector.tensor_copy(x3_bf16[:, cols], x_rows[3][:, cols])
+        nc.vector.tensor_copy(grouped[0][:, :, 3], x_rows[3][:].indirect(entries(offs_sb, 0, HALF)))
+        nc.scalar.activation(grouped[1][:, :, 3], x3_bf16[:].indirect(entries(offs_sb, HALF, HALF)), COPY)
+
+        accs = [[psum.tile([P, HALF], F32, name=f"y_acc{b}{h}") for h in range(N // P)] for b in range(2)]
+        quarter = HALF // 2
+        for b in range(2):
+            quantised = [
+                quantize(f"x{b}{i}", grouped[b][:, quarter * i : quarter * (i + 1), :], quarter) for i in range(2)
+            ]
+            for h in range(N // P):
+                for i in range(2):
+                    product(accs[b][h][:, quarter * i : quarter * (i + 1)], w1_sb, w1_plane, h, *quantised[i])
+        for b in range(2):
+            for h in range(N // P):
+                cols = slice(HALF * b, HALF * (b + 1))
+                result = keep.tile([P, HALF], F32, name=f"result{b}{h}")
+                nc.vector.tensor_tensor(result[:], accs[b][h][:], parents[b, h][:], ADD)
+                nc.sync.dma_start(out=out[P * h : P * (h + 1), cols], in_=result[:])

@@ -20,7 +20,6 @@ P = 128
 PACK = 4
 HALF = S // 2
 PAR_PIECE = 256
-LAST_CHUNKS = ((1024, "scalar"), (1024, "scalar"), (768, "scalar"), (512, "vector"), (512, "vector"), (256, "scalar"))
 
 
 def tile_picked_fpn_none_e_kernel(
@@ -61,17 +60,11 @@ def tile_picked_fpn_none_e_kernel(
         load_scales(w2_plane, w2_scales)
         nc.sync.dma_start(out=x_rows[0][:], in_=x_view[:, 0, :])
         nc.sync.dma_start(offs_sb[:], offs)
-        nc.sync.dma_start(out=w1_sb[:].bitcast(I32), in_=w1_words[0].bitcast(I32))
         nc.sync.dma_start(out=x_rows[1][:], in_=x_view[:, 1, :])
-        load_scales(w1_plane, w1_scales)
         nc.sync.dma_start(out=x_rows[2][:], in_=x_view[:, 2, :])
-        chunks = []
-        first = 0
-        for width, engine in LAST_CHUNKS:
-            cols = slice(first, first + width)
-            nc.sync.dma_start(out=x_rows[3][:, cols], in_=x_view[:, 3, cols])
-            chunks.append((cols, engine))
-            first = first + width
+        nc.sync.dma_start(out=x_rows[3][:], in_=x_view[:, 3, :])
+        nc.sync.dma_start(out=w1_sb[:].bitcast(I32), in_=w1_words[0].bitcast(I32))
+        load_scales(w1_plane, w1_scales)
 
         def quantize(name, grouped, width):
             codes = keep.tile([P, width], U32, name=name + "_codes", align_bytes=64)
@@ -135,30 +128,28 @@ def tile_picked_fpn_none_e_kernel(
                 picked01[:, :, HALF * b : HALF * (b + 1)].rearrange("p t c -> p c t"),
                 COPY,
             )
-        for b in (1, 0):
+        for b in range(2):
             nc.vector.tensor_copy(grouped[b][:, :, 2], x_rows[2][:].indirect(entries(offs_sb, HALF * b, HALF)))
 
-        x3_bf16 = keep.tile([P, T], BF16, name="x3_bf16")
-        for cols, engine in chunks:
-            if engine == "scalar":
-                nc.scalar.activation(x3_bf16[:, cols], x_rows[3][:, cols], COPY)
-            else:
-                nc.vector.tensor_copy(x3_bf16[:, cols], x_rows[3][:, cols])
-        nc.vector.tensor_copy(grouped[0][:, :, 3], x_rows[3][:].indirect(entries(offs_sb, 0, HALF)))
-        nc.scalar.activation(grouped[1][:, :, 3], x3_bf16[:].indirect(entries(offs_sb, HALF, HALF)), COPY)
+        quarter = HALF // 2
+        pieces = [(b, i) for b in range(2) for i in range(2)]
+        for b, i in pieces:
+            picked3 = keep.tile([P, quarter], BF16, name=f"picked3_{b}{i}")
+            nc.vector.tensor_copy(picked3[:], x_rows[3][:].indirect(entries(offs_sb, HALF * b + quarter * i, quarter)))
+            nc.scalar.activation(grouped[b][:, quarter * i : quarter * (i + 1), 3], picked3[:], COPY)
 
         accs = [[psum.tile([P, HALF], F32, name=f"y_acc{b}{h}") for h in range(N // P)] for b in range(2)]
-        quarter = HALF // 2
         for b in range(2):
             quantised = [
                 quantize(f"x{b}{i}", grouped[b][:, quarter * i : quarter * (i + 1), :], quarter) for i in range(2)
             ]
-            for h in range(N // P):
-                for i in range(2):
+            for i in range(2):
+                for h in range(N // P):
                     product(accs[b][h][:, quarter * i : quarter * (i + 1)], w1_sb, w1_plane, h, *quantised[i])
-        for b in range(2):
-            for h in range(N // P):
-                cols = slice(HALF * b, HALF * (b + 1))
-                result = keep.tile([P, HALF], F32, name=f"result{b}{h}")
-                nc.vector.tensor_tensor(result[:], accs[b][h][:], parents[b, h][:], ADD)
-                nc.sync.dma_start(out=out[P * h : P * (h + 1), cols], in_=result[:])
+        for b, h, first, width in (
+            (0, 0, 0, HALF), (0, 1, 0, HALF), (1, 0, 0, HALF), (1, 1, 0, quarter), (1, 1, quarter, quarter)
+        ):
+            cols = slice(first, first + width)
+            result = keep.tile([P, width], F32, name=f"result{b}{h}{first}")
+            nc.vector.tensor_tensor(result[:], accs[b][h][:, cols], parents[b, h][:, cols], ADD)
+            nc.sync.dma_start(out=out[P * h : P * (h + 1), HALF * b + first : HALF * b + first + width], in_=result[:])

@@ -19,7 +19,8 @@ ADD = mybir.AluOpType.add
 P = 128
 PACK = 4
 HALF = S // 2
-PAR_PIECE = 256
+PIECE = 256
+PIECES = S // PIECE
 
 
 def tile_picked_fpn_none_e_kernel(
@@ -28,6 +29,8 @@ def tile_picked_fpn_none_e_kernel(
     nc = tc.nc
     with ExitStack() as ctx:
         keep = ctx.enter_context(tc.tile_pool(name="keep", bufs=1))
+        ring = ctx.enter_context(tc.tile_pool(name="ring", bufs=3))
+        pair = ctx.enter_context(tc.tile_pool(name="pair", bufs=2))
         psum = ctx.enter_context(tc.psum_pool(name="psum", bufs=1))
 
         offs_sb = keep.tile([P, S // 16], U16, name="offs_sb")
@@ -66,8 +69,8 @@ def tile_picked_fpn_none_e_kernel(
         nc.sync.dma_start(out=w1_sb[:].bitcast(I32), in_=w1_words[0].bitcast(I32))
         load_scales(w1_plane, w1_scales)
 
-        def quantize(name, grouped, width):
-            codes = keep.tile([P, width], U32, name=name + "_codes", align_bytes=64)
+        def quantize(name, grouped, width, pool=keep, tag=None):
+            codes = pool.tile([P, width], U32, name=name + "_codes", tag=tag or name + "_codes", align_bytes=64)
             scales = keep.tile([P, width], U8, name=name + "_scales", align_bytes=64)
             nc.vector.quantize_mx(
                 out=codes[:].bitcast(FP8X4), scales=scales[:], in_=grouped.rearrange("p c t -> p (c t)")
@@ -105,23 +108,20 @@ def tile_picked_fpn_none_e_kernel(
 
         parents = {}
 
-        def fetch_parents(b, h, tag):
-            parent = keep.tile([P, HALF], F32, name=f"parent{b}{h}", tag=tag)
-            for first in range(0, HALF, PAR_PIECE):
-                nc.vector.tensor_copy(
-                    parent[:, first : first + PAR_PIECE],
-                    t_sbs[h][:].indirect(entries(par_sb, HALF * b + first, PAR_PIECE)),
-                )
-            parents[b, h] = parent
+        def fetch_parents(piece, tag):
+            parent = keep.tile([P, N // P, PIECE], F32, name=f"parent{piece}", tag=tag)
+            for h in range(N // P):
+                nc.vector.tensor_copy(parent[:, h, :], t_sbs[h][:].indirect(entries(par_sb, PIECE * piece, PIECE)))
+            parents[piece] = parent
 
-        for b, h in ((0, 0), (1, 0), (0, 1)):
-            fetch_parents(b, h, f"parent{b}{h}")
+        for piece in range(PIECES - 1):
+            fetch_parents(piece, f"parent{piece}")
 
         grouped = [keep.tile([P, HALF, PACK], BF16, name=f"grouped{b}", align_bytes=64) for b in range(2)]
         picked01 = keep.tile([P, 2, S], BF16, name="picked01")
         for t in range(2):
             nc.vector.tensor_copy(picked01[:, t, :], x_rows[t][:].indirect(offs_sb[:]))
-        fetch_parents(1, 1, "x_row1")
+        fetch_parents(PIECES - 1, "x_row1")
         for b in range(2):
             nc.scalar.activation(
                 grouped[b][:, :, 0:2],
@@ -131,25 +131,41 @@ def tile_picked_fpn_none_e_kernel(
         for b in range(2):
             nc.vector.tensor_copy(grouped[b][:, :, 2], x_rows[2][:].indirect(entries(offs_sb, HALF * b, HALF)))
 
-        quarter = HALF // 2
-        pieces = [(b, i) for b in range(2) for i in range(2)]
-        for b, i in pieces:
-            picked3 = keep.tile([P, quarter], BF16, name=f"picked3_{b}{i}")
-            nc.vector.tensor_copy(picked3[:], x_rows[3][:].indirect(entries(offs_sb, HALF * b + quarter * i, quarter)))
-            nc.scalar.activation(grouped[b][:, quarter * i : quarter * (i + 1), 3], picked3[:], COPY)
+        out_view = out.rearrange("(h p) j -> p h j", p=P)
 
-        accs = [[psum.tile([P, HALF], F32, name=f"y_acc{b}{h}") for h in range(N // P)] for b in range(2)]
-        for b in range(2):
-            quantised = [
-                quantize(f"x{b}{i}", grouped[b][:, quarter * i : quarter * (i + 1), :], quarter) for i in range(2)
-            ]
-            for i in range(2):
-                for h in range(N // P):
-                    product(accs[b][h][:, quarter * i : quarter * (i + 1)], w1_sb, w1_plane, h, *quantised[i])
-        for b, h, first, width in (
-            (0, 0, 0, HALF), (0, 1, 0, HALF), (1, 0, 0, HALF), (1, 1, 0, quarter), (1, 1, quarter, quarter)
-        ):
-            cols = slice(first, first + width)
-            result = keep.tile([P, width], F32, name=f"result{b}{h}{first}")
-            nc.vector.tensor_tensor(result[:], accs[b][h][:, cols], parents[b, h][:, cols], ADD)
-            nc.sync.dma_start(out=out[P * h : P * (h + 1), HALF * b + first : HALF * b + first + width], in_=result[:])
+        def slot(piece):
+            first = PIECE * piece % HALF
+            return grouped[PIECE * piece // HALF][:, first : first + PIECE, :]
+
+        def pick(piece):
+            picked3 = ring.tile([P, PIECE], BF16, name="picked3")
+            nc.vector.tensor_copy(picked3[:], x_rows[3][:].indirect(entries(offs_sb, PIECE * piece, PIECE)))
+            nc.scalar.activation(slot(piece)[:, :, 3], picked3[:], COPY)
+
+        accs = {}
+
+        def multiply(piece):
+            quantised = quantize(f"x{piece}", slot(piece), PIECE, pair, "x_codes")
+            for halves in ([0, 1],) if piece < PIECES - 1 else ([0], [1]):
+                acc = psum.tile([P, len(halves), PIECE], F32, name=f"y_acc{piece}{halves[0]}")
+                for i, h in enumerate(halves):
+                    product(acc[:, i, :], w1_sb, w1_plane, h, *quantised)
+                accs.setdefault(piece, []).append((halves, acc))
+
+        def add_and_store(piece):
+            for halves, acc in accs[piece]:
+                rows = slice(halves[0], halves[-1] + 1)
+                result = keep.tile([P, len(halves), PIECE], F32, name=f"result{piece}{halves[0]}")
+                nc.vector.tensor_tensor(result[:], acc[:], parents[piece][:, rows, :], ADD)
+                nc.sync.dma_start(out=out_view[:, rows, PIECE * piece : PIECE * (piece + 1)], in_=result[:])
+
+        for piece in range(PIECES - 1):
+            pick(piece)
+        multiply(0)
+        pick(3)
+        multiply(1)
+        add_and_store(0)
+        multiply(2)
+        multiply(3)
+        for piece in range(1, PIECES):
+            add_and_store(piece)

@@ -114,28 +114,29 @@ def tile_picked_fpn_none_e_kernel(
                 nc.vector.tensor_copy(parent[:, h, :], t_sbs[h][:].indirect(entries(par_sb, PIECE * piece, PIECE)))
             parents[piece] = parent
 
-        for piece in range(PIECES - 1):
-            fetch_parents(piece, f"parent{piece}")
-
         grouped = [keep.tile([P, HALF, PACK], BF16, name=f"grouped{b}", align_bytes=64) for b in range(2)]
-        picked01 = keep.tile([P, 2, S], BF16, name="picked01")
-        for t in range(2):
-            nc.vector.tensor_copy(picked01[:, t, :], x_rows[t][:].indirect(offs_sb[:]))
-        fetch_parents(PIECES - 1, "x_row1")
-        for b in range(2):
-            nc.scalar.activation(
-                grouped[b][:, :, 0:2],
-                picked01[:, :, HALF * b : HALF * (b + 1)].rearrange("p t c -> p c t"),
-                COPY,
-            )
-        for b in range(2):
-            nc.vector.tensor_copy(grouped[b][:, :, 2], x_rows[2][:].indirect(entries(offs_sb, HALF * b, HALF)))
-
-        out_view = out.rearrange("(h p) j -> p h j", p=P)
 
         def slot(piece):
             first = PIECE * piece % HALF
             return grouped[PIECE * piece // HALF][:, first : first + PIECE, :]
+
+        fetch_parents(0, "parent0")
+        fetch_parents(1, "parent1")
+        for t in range(2):
+            for b in range(2):
+                picked = keep.tile([P, HALF], BF16, name=f"picked{t}{b}")
+                nc.vector.tensor_copy(picked[:], x_rows[t][:].indirect(entries(offs_sb, HALF * b, HALF)))
+                nc.scalar.activation(grouped[b][:, :, t], picked[:], COPY)
+            fetch_parents(2 + t, f"x_row{t}")
+        for piece in range(PIECES):
+            picked = keep.tile([P, PIECE], BF16, name=f"picked2{piece}")
+            nc.vector.tensor_copy(picked[:], x_rows[2][:].indirect(entries(offs_sb, PIECE * piece, PIECE)))
+            if piece < PIECES - 1:
+                nc.scalar.activation(slot(piece)[:, :, 2], picked[:], COPY)
+            else:
+                nc.vector.tensor_copy(slot(piece)[:, :, 2], picked[:])
+
+        out_view = out.rearrange("(h p) j -> p h j", p=P)
 
         def pick(piece):
             picked3 = ring.tile([P, PIECE], BF16, name="picked3")
@@ -166,6 +167,7 @@ def tile_picked_fpn_none_e_kernel(
         multiply(1)
         add_and_store(0)
         multiply(2)
+        add_and_store(1)
         multiply(3)
-        for piece in range(1, PIECES):
+        for piece in range(2, PIECES):
             add_and_store(piece)

@@ -153,21 +153,26 @@ def tile_picked_fpn_none_e_kernel(
                     product(acc[:, i, :], w1_sb, w1_plane, h, *quantised)
                 accs.setdefault(piece, []).append((halves, acc))
 
-        def add_and_store(piece):
+        def add_and_store(piece, rows):
             for halves, acc in accs[piece]:
-                rows = slice(halves[0], halves[-1] + 1)
-                result = keep.tile([P, len(halves), PIECE], F32, name=f"result{piece}{halves[0]}")
-                nc.vector.tensor_tensor(result[:], acc[:], parents[piece][:, rows, :], ADD)
-                nc.sync.dma_start(out=out_view[:, rows, PIECE * piece : PIECE * (piece + 1)], in_=result[:])
+                if rows[0] in halves:
+                    within = slice(rows[0] - halves[0], rows[-1] - halves[0] + 1)
+                    rows = slice(rows[0], rows[-1] + 1)
+                    result = keep.tile([P, rows.stop - rows.start, PIECE], F32, name=f"result{piece}{rows.start}")
+                    nc.vector.tensor_tensor(result[:], acc[:, within, :], parents[piece][:, rows, :], ADD)
+                    nc.sync.dma_start(out=out_view[:, rows, PIECE * piece : PIECE * (piece + 1)], in_=result[:])
+                    return
 
         for piece in range(PIECES - 1):
             pick(piece)
         multiply(0)
         pick(3)
         multiply(1)
-        add_and_store(0)
+        add_and_store(0, [0, 1])
         multiply(2)
-        add_and_store(1)
+        add_and_store(1, [0])
         multiply(3)
+        add_and_store(1, [1])
         for piece in range(2, PIECES):
-            add_and_store(piece)
+            for h in range(N // P):
+                add_and_store(piece, [h])

@@ -138,41 +138,40 @@ def tile_picked_fpn_none_e_kernel(
 
         out_view = out.rearrange("(h p) j -> p h j", p=P)
 
-        def pick(piece):
+        def pick(piece, parts=1):
+            width = PIECE // parts
             picked3 = ring.tile([P, PIECE], BF16, name="picked3")
-            nc.vector.tensor_copy(picked3[:], x_rows[3][:].indirect(entries(offs_sb, PIECE * piece, PIECE)))
-            nc.scalar.activation(slot(piece)[:, :, 3], picked3[:], COPY)
+            for first in range(0, PIECE, width):
+                part = picked3[:, first : first + width]
+                nc.vector.tensor_copy(part, x_rows[3][:].indirect(entries(offs_sb, PIECE * piece + first, width)))
+                nc.scalar.activation(slot(piece)[:, first : first + width, 3], part, COPY)
 
         accs = {}
 
         def multiply(piece):
             quantised = quantize(f"x{piece}", slot(piece), PIECE, pair, "x_codes")
-            for halves in ([0, 1],) if piece < PIECES - 1 else ([0], [1]):
-                acc = psum.tile([P, len(halves), PIECE], F32, name=f"y_acc{piece}{halves[0]}")
-                for i, h in enumerate(halves):
-                    product(acc[:, i, :], w1_sb, w1_plane, h, *quantised)
-                accs.setdefault(piece, []).append((halves, acc))
+            for h in range(N // P):
+                tag = f"t_acc{h}" if piece == PIECES - 1 else f"y_acc{piece}{h}"
+                accs[piece, h] = psum.tile([P, PIECE], F32, name=f"y_acc{piece}{h}", tag=tag)
+                product(accs[piece, h][:], w1_sb, w1_plane, h, *quantised)
 
-        def add_and_store(piece, rows):
-            for halves, acc in accs[piece]:
-                if rows[0] in halves:
-                    within = slice(rows[0] - halves[0], rows[-1] - halves[0] + 1)
-                    rows = slice(rows[0], rows[-1] + 1)
-                    result = keep.tile([P, rows.stop - rows.start, PIECE], F32, name=f"result{piece}{rows.start}")
-                    nc.vector.tensor_tensor(result[:], acc[:, within, :], parents[piece][:, rows, :], ADD)
-                    nc.sync.dma_start(out=out_view[:, rows, PIECE * piece : PIECE * (piece + 1)], in_=result[:])
-                    return
+        def add_and_store(piece, h):
+            result = keep.tile([P, PIECE], F32, name=f"result{piece}{h}")
+            nc.vector.tensor_tensor(result[:], accs[piece, h][:], parents[piece][:, h, :], ADD)
+            nc.sync.dma_start(out=out_view[:, h, PIECE * piece : PIECE * (piece + 1)], in_=result[:])
 
-        for piece in range(PIECES - 1):
-            pick(piece)
+        pick(0, parts=2)
+        pick(1)
+        pick(2)
         multiply(0)
         pick(3)
         multiply(1)
-        add_and_store(0, [0, 1])
+        add_and_store(0, 0)
+        add_and_store(0, 1)
         multiply(2)
-        add_and_store(1, [0])
+        add_and_store(1, 0)
         multiply(3)
-        add_and_store(1, [1])
+        add_and_store(1, 1)
         for piece in range(2, PIECES):
             for h in range(N // P):
-                add_and_store(piece, [h])
+                add_and_store(piece, h)

@@ -166,8 +166,10 @@ def tile_picked_fpn_none_e_kernel(
         multiply(0)
         pick(3)
         multiply(1)
-        add_and_store(0, 0)
-        add_and_store(0, 1)
+        first_result = keep.tile([P, N // P, PIECE], F32, name="first_result")
+        for h in range(N // P):
+            nc.vector.tensor_tensor(first_result[:, h, :], accs[0, h][:], parents[0][:, h, :], ADD)
+        nc.sync.dma_start(out=out_view[:, :, 0:PIECE], in_=first_result[:])
         multiply(2)
         add_and_store(1, 0)
         multiply(3)

@@ -13,7 +13,6 @@ U16 = mybir.dt.uint16
 U8 = mybir.dt.uint8
 FP8X4 = mybir.dt.float8_e4m3fn_x4
 FP4X4 = mybir.dt.float4_e2m1fn_x4
-COPY = mybir.ActivationFunctionType.Copy
 ADD = mybir.AluOpType.add
 
 P = 128
@@ -95,7 +94,7 @@ def tile_picked_fpn_none_e_kernel(
             if b == 0:
                 nc.vector.tensor_copy(out=s_grouped[:], in_=cells)
             else:
-                nc.scalar.activation(s_grouped[:], cells, COPY)
+                nc.scalar.copy(s_grouped[:], cells)
             s_quantised.append(quantize(f"s{b}", s_grouped[:], V // 2))
         t_sbs = []
         for h in range(N // P):
@@ -103,7 +102,7 @@ def tile_picked_fpn_none_e_kernel(
             for b in range(2):
                 product(t_acc[:, V // 2 * b : V // 2 * (b + 1)], w2_sb, w2_plane, h, *s_quantised[b])
             t_sb = keep.tile([P, V], F32, name=f"t_sb{h}")
-            nc.scalar.activation(t_sb[:], t_acc[:], COPY)
+            nc.scalar.copy(t_sb[:], t_acc[:])
             t_sbs.append(t_sb)
 
         parents = {}
@@ -126,13 +125,13 @@ def tile_picked_fpn_none_e_kernel(
             for b in range(2):
                 picked = keep.tile([P, HALF], BF16, name=f"picked{t}{b}")
                 nc.vector.tensor_copy(picked[:], x_rows[t][:].indirect(entries(offs_sb, HALF * b, HALF)))
-                nc.scalar.activation(grouped[b][:, :, t], picked[:], COPY)
+                nc.scalar.copy(grouped[b][:, :, t], picked[:])
             fetch_parents(2 + t, f"x_row{t}")
         for piece in range(PIECES):
             picked = keep.tile([P, PIECE], BF16, name=f"picked2{piece}")
             nc.vector.tensor_copy(picked[:], x_rows[2][:].indirect(entries(offs_sb, PIECE * piece, PIECE)))
             if piece < PIECES - 1:
-                nc.scalar.activation(slot(piece)[:, :, 2], picked[:], COPY)
+                nc.scalar.copy(slot(piece)[:, :, 2], picked[:])
             else:
                 nc.vector.tensor_copy(slot(piece)[:, :, 2], picked[:])
 
@@ -144,7 +143,7 @@ def tile_picked_fpn_none_e_kernel(
             for first in range(0, PIECE, width):
                 part = picked3[:, first : first + width]
                 nc.vector.tensor_copy(part, x_rows[3][:].indirect(entries(offs_sb, PIECE * piece + first, width)))
-                nc.scalar.activation(slot(piece)[:, first : first + width, 3], part, COPY)
+                nc.scalar.copy(slot(piece)[:, first : first + width, 3], part)
 
         accs = {}
 

@@ -171,8 +171,8 @@ def tile_picked_fpn_none_e_kernel(
         nc.sync.dma_start(out=out_view[:, :, 0:PIECE], in_=first_result[:])
         multiply(2)
         add_and_store(1, 0)
-        multiply(3)
         add_and_store(1, 1)
+        multiply(3)
         for piece in range(2, PIECES):
             for h in range(N // P):
                 add_and_store(piece, h)

@@ -29,7 +29,6 @@ def tile_picked_fpn_none_e_kernel(
     with ExitStack() as ctx:
         keep = ctx.enter_context(tc.tile_pool(name="keep", bufs=1))
         ring = ctx.enter_context(tc.tile_pool(name="ring", bufs=3))
-        pair = ctx.enter_context(tc.tile_pool(name="pair", bufs=2))
         psum = ctx.enter_context(tc.psum_pool(name="psum", bufs=1))
 
         offs_sb = keep.tile([P, S // 16], U16, name="offs_sb")
@@ -147,8 +146,8 @@ def tile_picked_fpn_none_e_kernel(
 
         accs = {}
 
-        def multiply(piece):
-            quantised = quantize(f"x{piece}", slot(piece), PIECE, pair, "x_codes")
+        def multiply(piece, codes_tag):
+            quantised = quantize(f"x{piece}", slot(piece), PIECE, keep, codes_tag)
             for h in range(N // P):
                 tag = f"t_acc{h}" if piece == PIECES - 1 else f"y_acc{piece}{h}"
                 accs[piece, h] = psum.tile([P, PIECE], F32, name=f"y_acc{piece}{h}", tag=tag)
@@ -162,17 +161,17 @@ def tile_picked_fpn_none_e_kernel(
         pick(0, parts=2)
         pick(1)
         pick(2)
-        multiply(0)
+        multiply(0, "codes0")
         pick(3)
-        multiply(1)
+        multiply(1, "codes1")
         first_result = keep.tile([P, N // P, PIECE], F32, name="first_result")
         for h in range(N // P):
             nc.vector.tensor_tensor(first_result[:, h, :], accs[0, h][:], parents[0][:, h, :], ADD)
         nc.sync.dma_start(out=out_view[:, :, 0:PIECE], in_=first_result[:])
-        multiply(2)
+        multiply(2, "codes0")
         add_and_store(1, 0)
+        multiply(3, "x0_scales")
         add_and_store(1, 1)
-        multiply(3)
         for piece in range(2, PIECES):
             for h in range(N // P):
                 add_and_store(piece, h)

@@ -14,6 +14,7 @@ U8 = mybir.dt.uint8
 FP8X4 = mybir.dt.float8_e4m3fn_x4
 FP4X4 = mybir.dt.float4_e2m1fn_x4
 ADD = mybir.AluOpType.add
+COPY = mybir.ActivationFunctionType.Copy
 
 P = 128
 PACK = 4
@@ -28,7 +29,6 @@ def tile_picked_fpn_none_e_kernel(
     nc = tc.nc
     with ExitStack() as ctx:
         keep = ctx.enter_context(tc.tile_pool(name="keep", bufs=1))
-        ring = ctx.enter_context(tc.tile_pool(name="ring", bufs=3))
         psum = ctx.enter_context(tc.psum_pool(name="psum", bufs=1))
 
         offs_sb = keep.tile([P, S // 16], U16, name="offs_sb")
@@ -101,7 +101,7 @@ def tile_picked_fpn_none_e_kernel(
             for b in range(2):
                 product(t_acc[:, V // 2 * b : V // 2 * (b + 1)], w2_sb, w2_plane, h, *s_quantised[b])
             t_sb = keep.tile([P, V], F32, name=f"t_sb{h}")
-            nc.scalar.copy(t_sb[:], t_acc[:])
+            nc.scalar.activation(t_sb[:], t_acc[:], COPY)
             t_sbs.append(t_sb)
 
         parents = {}
@@ -114,63 +114,74 @@ def tile_picked_fpn_none_e_kernel(
 
         grouped = [keep.tile([P, HALF, PACK], BF16, name=f"grouped{b}", align_bytes=64) for b in range(2)]
 
-        def slot(piece):
-            first = PIECE * piece % HALF
-            return grouped[PIECE * piece // HALF][:, first : first + PIECE, :]
+        def slot(first, count):
+            return grouped[first // HALF][:, first % HALF : first % HALF + count, :]
 
         fetch_parents(0, "parent0")
         fetch_parents(1, "parent1")
         for t in range(2):
             for b in range(2):
                 picked = keep.tile([P, HALF], BF16, name=f"picked{t}{b}")
-                nc.vector.tensor_copy(picked[:], x_rows[t][:].indirect(entries(offs_sb, HALF * b, HALF)))
+                cells = x_rows[t][:].indirect(entries(offs_sb, HALF * b, HALF))
+                if (t, b) == (0, 1):
+                    nc.scalar.activation(picked[:], cells, COPY)
+                else:
+                    nc.vector.tensor_copy(picked[:], cells)
                 nc.scalar.copy(grouped[b][:, :, t], picked[:])
             fetch_parents(2 + t, f"x_row{t}")
         for piece in range(PIECES):
             picked = keep.tile([P, PIECE], BF16, name=f"picked2{piece}")
             nc.vector.tensor_copy(picked[:], x_rows[2][:].indirect(entries(offs_sb, PIECE * piece, PIECE)))
-            if piece < PIECES - 1:
-                nc.scalar.copy(slot(piece)[:, :, 2], picked[:])
+            if piece == 0:
+                nc.vector.tensor_copy(slot(0, PIECE)[:, :, 2], picked[:])
             else:
-                nc.vector.tensor_copy(slot(piece)[:, :, 2], picked[:])
+                nc.scalar.copy(slot(PIECE * piece, PIECE)[:, :, 2], picked[:])
 
         out_view = out.rearrange("(h p) j -> p h j", p=P)
+        last = keep.tile([P, S], BF16, name="last")
+        part = PIECE // 2
 
-        def pick(piece, parts=1):
-            width = PIECE // parts
-            picked3 = ring.tile([P, PIECE], BF16, name="picked3")
-            for first in range(0, PIECE, width):
-                part = picked3[:, first : first + width]
-                nc.vector.tensor_copy(part, x_rows[3][:].indirect(entries(offs_sb, PIECE * piece + first, width)))
-                nc.scalar.copy(slot(piece)[:, first : first + width, 3], part)
+        def window(first, count):
+            return x_rows[3][:].indirect(entries(offs_sb, first, count))
+
+        def weave(copy, first, count):
+            copy(slot(first, count)[:, :, 3], last[:, first : first + count])
 
         accs = {}
-
-        def multiply(piece, codes_tag):
-            quantised = quantize(f"x{piece}", slot(piece), PIECE, keep, codes_tag)
+        for piece in range(PIECES):
             for h in range(N // P):
                 tag = f"t_acc{h}" if piece == PIECES - 1 else f"y_acc{piece}{h}"
                 accs[piece, h] = psum.tile([P, PIECE], F32, name=f"y_acc{piece}{h}", tag=tag)
-                product(accs[piece, h][:], w1_sb, w1_plane, h, *quantised)
+
+        def multiply(first, count, codes_tag=None):
+            quantised = quantize(f"x{first}", slot(first, count), count, keep, codes_tag)
+            at = first % PIECE
+            for h in range(N // P):
+                product(accs[first // PIECE, h][:, at : at + count], w1_sb, w1_plane, h, *quantised)
 
         def add_and_store(piece, h):
             result = keep.tile([P, PIECE], F32, name=f"result{piece}{h}")
             nc.vector.tensor_tensor(result[:], accs[piece, h][:], parents[piece][:, h, :], ADD)
             nc.sync.dma_start(out=out_view[:, h, PIECE * piece : PIECE * (piece + 1)], in_=result[:])
 
-        pick(0, parts=2)
-        pick(1)
-        pick(2)
-        multiply(0, "codes0")
-        pick(3)
-        multiply(1, "codes1")
-        first_result = keep.tile([P, N // P, PIECE], F32, name="first_result")
-        for h in range(N // P):
-            nc.vector.tensor_tensor(first_result[:, h, :], accs[0, h][:], parents[0][:, h, :], ADD)
-        nc.sync.dma_start(out=out_view[:, :, 0:PIECE], in_=first_result[:])
-        multiply(2, "codes0")
+        for first in (0, part):
+            nc.vector.tensor_copy(last[:, first : first + part], window(first, part))
+        for first in range(PIECE, S, PIECE):
+            nc.scalar.activation(last[:, first : first + PIECE], window(first, PIECE), COPY)
+        for first in range(0, 3 * part, part):
+            weave(nc.vector.tensor_copy, first, part)
+        multiply(0, PIECE)
+        for first in (3 * part, 4 * part):
+            weave(nc.vector.tensor_copy, first, part)
+        weave(nc.scalar.copy, 5 * part, part)
+        weave(nc.scalar.copy, 6 * part, PIECE)
+        multiply(PIECE, PIECE)
+        multiply(4 * part, part)
+        add_and_store(0, 0)
+        multiply(5 * part, part)
+        add_and_store(0, 1)
         add_and_store(1, 0)
-        multiply(3, "x0_scales")
+        multiply(6 * part, PIECE, "x0_codes")
         add_and_store(1, 1)
         for piece in range(2, PIECES):
             for h in range(N // P):

@@ -177,11 +177,13 @@ def tile_picked_fpn_none_e_kernel(
         weave(nc.scalar.copy, 6 * part, PIECE)
         multiply(PIECE, PIECE)
         multiply(4 * part, part)
-        add_and_store(0, 0)
-        multiply(5 * part, part)
-        add_and_store(0, 1)
+        first_result = keep.tile([P, N // P, PIECE], F32, name="first_result")
+        for h in range(N // P):
+            nc.vector.tensor_tensor(first_result[:, h, :], accs[0, h][:], parents[0][:, h, :], ADD)
+        nc.sync.dma_start(out=out_view[:, :, 0:PIECE], in_=first_result[:])
+        multiply(5 * part, part, "x0_codes")
         add_and_store(1, 0)
-        multiply(6 * part, PIECE, "x0_codes")
+        multiply(6 * part, PIECE, "x0_scales")
         add_and_store(1, 1)
         for piece in range(2, PIECES):
             for h in range(N // P):

@@ -52,16 +52,16 @@ def tile_picked_fpn_none_e_kernel(
         s_raw = keep.tile([P, PACK, V], F32, name="s_raw")
         w2_sb = keep.tile([P, 2 * N], U8, name="w2_sb", align_bytes=64)
         w1_sb = keep.tile([P, 2 * N], U8, name="w1_sb", align_bytes=64)
-        x_rows = [keep.tile([P, T], F32, name=f"x_row{t}", tag=f"x_row{t}") for t in range(PACK)]
+        x_pair = keep.tile([P, 2, T], F32, name="x_pair")
+        x_rows = {t: keep.tile([P, T], F32, name=f"x_row{t}") for t in (2, 3)}
         x_view = xT.rearrange("(p t) c -> p t c", t=PACK)
 
         nc.sync.dma_start(out=s_raw[:], in_=sT.rearrange("(p t) v -> p t v", t=PACK))
         nc.sync.dma_start(out=w2_sb[:].bitcast(I32), in_=w2_words[0].bitcast(I32))
         nc.sync.dma_start(par_sb[:], par)
         load_scales(w2_plane, w2_scales)
-        nc.sync.dma_start(out=x_rows[0][:], in_=x_view[:, 0, :])
+        nc.sync.dma_start(out=x_pair[:], in_=x_view[:, 0:2, :])
         nc.sync.dma_start(offs_sb[:], offs)
-        nc.sync.dma_start(out=x_rows[1][:], in_=x_view[:, 1, :])
         nc.sync.dma_start(out=x_rows[2][:], in_=x_view[:, 2, :])
         nc.sync.dma_start(out=x_rows[3][:], in_=x_view[:, 3, :])
         nc.sync.dma_start(out=w1_sb[:].bitcast(I32), in_=w1_words[0].bitcast(I32))
@@ -106,8 +106,8 @@ def tile_picked_fpn_none_e_kernel(
 
         parents = {}
 
-        def fetch_parents(piece, tag):
-            parent = keep.tile([P, N // P, PIECE], F32, name=f"parent{piece}", tag=tag)
+        def fetch_parents(piece):
+            parent = keep.tile([P, N // P, PIECE], F32, name=f"parent{piece}")
             for h in range(N // P):
                 nc.vector.tensor_copy(parent[:, h, :], t_sbs[h][:].indirect(entries(par_sb, PIECE * piece, PIECE)))
             parents[piece] = parent
@@ -117,29 +117,22 @@ def tile_picked_fpn_none_e_kernel(
         def slot(first, count):
             return grouped[first // HALF][:, first % HALF : first % HALF + count, :]
 
-        fetch_parents(0, "parent0")
-        fetch_parents(1, "parent1")
-        for t in range(2):
-            for b in range(2):
-                picked = keep.tile([P, HALF], BF16, name=f"picked{t}{b}")
-                cells = x_rows[t][:].indirect(entries(offs_sb, HALF * b, HALF))
-                if (t, b) == (0, 1):
-                    nc.scalar.activation(picked[:], cells, COPY)
-                else:
-                    nc.vector.tensor_copy(picked[:], cells)
-                nc.scalar.copy(grouped[b][:, :, t], picked[:])
-            fetch_parents(2 + t, f"x_row{t}")
         for piece in range(PIECES):
-            picked = keep.tile([P, PIECE], BF16, name=f"picked2{piece}")
-            nc.vector.tensor_copy(picked[:], x_rows[2][:].indirect(entries(offs_sb, PIECE * piece, PIECE)))
-            if piece == 0:
-                nc.vector.tensor_copy(slot(0, PIECE)[:, :, 2], picked[:])
-            else:
-                nc.scalar.copy(slot(PIECE * piece, PIECE)[:, :, 2], picked[:])
+            fetch_parents(piece)
+        picked01 = keep.tile([P, 2, HALF], F32, name="picked01")
+        for t in range(2):
+            nc.vector.tensor_copy(grouped[0][:, :, t], x_pair[:, t, :].indirect(entries(offs_sb, 0, HALF)))
+            nc.scalar.activation(picked01[:, t, :], x_pair[:, t, :].indirect(entries(offs_sb, HALF, HALF)), COPY)
+        nc.scalar.copy(grouped[1][:, :, 0:2], picked01[:].rearrange("p t j -> p j t"))
+        part = PIECE // 2
+        picked2 = keep.tile([P, S], BF16, name="picked2")
+        for first in range(0, S, PIECE):
+            nc.vector.tensor_copy(picked2[:, first : first + PIECE], x_rows[2][:].indirect(entries(offs_sb, first, PIECE)))
+            copy = nc.scalar.copy if first < S - PIECE else nc.vector.tensor_copy
+            copy(slot(first, PIECE)[:, :, 2], picked2[:, first : first + PIECE])
 
         out_view = out.rearrange("(h p) j -> p h j", p=P)
         last = keep.tile([P, S], BF16, name="last")
-        part = PIECE // 2
 
         def window(first, count):
             return x_rows[3][:].indirect(entries(offs_sb, first, count))
@@ -159,32 +152,34 @@ def tile_picked_fpn_none_e_kernel(
             for h in range(N // P):
                 product(accs[first // PIECE, h][:, at : at + count], w1_sb, w1_plane, h, *quantised)
 
-        def add_and_store(piece, h):
-            result = keep.tile([P, PIECE], F32, name=f"result{piece}{h}")
-            nc.vector.tensor_tensor(result[:], accs[piece, h][:], parents[piece][:, h, :], ADD)
-            nc.sync.dma_start(out=out_view[:, h, PIECE * piece : PIECE * (piece + 1)], in_=result[:])
+        def add_and_store(h, *pieces):
+            result = keep.tile([P, len(pieces), PIECE], F32, name=f"result{pieces[0]}{h}")
+            for i, piece in enumerate(pieces):
+                nc.vector.tensor_tensor(result[:, i, :], accs[piece, h][:], parents[piece][:, h, :], ADD)
+            nc.sync.dma_start(
+                out=out_view[:, h, PIECE * pieces[0] : PIECE * (pieces[-1] + 1)],
+                in_=result[:].rearrange("p i j -> p (i j)"),
+            )
 
-        for first in (0, part):
-            nc.vector.tensor_copy(last[:, first : first + part], window(first, part))
-        for first in range(PIECE, S, PIECE):
-            nc.scalar.activation(last[:, first : first + PIECE], window(first, PIECE), COPY)
-        for first in range(0, 3 * part, part):
-            weave(nc.vector.tensor_copy, first, part)
+        for first, count in ((PIECE, PIECE), (7 * part, part)):
+            nc.vector.tensor_copy(last[:, first : first + count], window(first, count))
+        for first, count in ((0, PIECE), (4 * part, part), (5 * part, part)):
+            nc.scalar.activation(last[:, first : first + count], window(first, count), COPY)
+        weave(nc.scalar.copy, PIECE, PIECE)
+        nc.scalar.activation(last[:, 6 * part : 7 * part], window(6 * part, part), COPY)
+        weave(nc.scalar.copy, 7 * part, part)
+        weave(nc.scalar.copy, 6 * part, part)
+        weave(nc.vector.tensor_copy, 0, PIECE)
+        weave(nc.vector.tensor_copy, 4 * part, part)
         multiply(0, PIECE)
-        for first in (3 * part, 4 * part):
-            weave(nc.vector.tensor_copy, first, part)
-        weave(nc.scalar.copy, 5 * part, part)
-        weave(nc.scalar.copy, 6 * part, PIECE)
+        weave(nc.vector.tensor_copy, 5 * part, part)
         multiply(PIECE, PIECE)
-        multiply(4 * part, part)
-        first_result = keep.tile([P, N // P, PIECE], F32, name="first_result")
-        for h in range(N // P):
-            nc.vector.tensor_tensor(first_result[:, h, :], accs[0, h][:], parents[0][:, h, :], ADD)
-        nc.sync.dma_start(out=out_view[:, :, 0:PIECE], in_=first_result[:])
-        multiply(5 * part, part, "x0_codes")
+        multiply(2 * PIECE, PIECE)
+        add_and_store(0, 0)
         add_and_store(1, 0)
-        multiply(6 * part, PIECE, "x0_scales")
+        add_and_store(0, 1)
+        multiply(6 * part, PIECE, "x0_codes")
         add_and_store(1, 1)
-        for piece in range(2, PIECES):
+        for piece in (2, 3):
             for h in range(N // P):
-                add_and_store(piece, h)
+                add_and_store(h, piece)

@@ -126,9 +126,9 @@ def tile_picked_fpn_none_e_kernel(
         nc.scalar.copy(grouped[1][:, :, 0:2], picked01[:].rearrange("p t j -> p j t"))
         part = PIECE // 2
         picked2 = keep.tile([P, S], BF16, name="picked2")
-        for first in range(0, S, PIECE):
+        for first in reversed(range(0, S, PIECE)):
             nc.vector.tensor_copy(picked2[:, first : first + PIECE], x_rows[2][:].indirect(entries(offs_sb, first, PIECE)))
-            copy = nc.scalar.copy if first < S - PIECE else nc.vector.tensor_copy
+            copy = nc.scalar.copy if first > 0 else nc.vector.tensor_copy
             copy(slot(first, PIECE)[:, :, 2], picked2[:, first : first + PIECE])
 
         out_view = out.rearrange("(h p) j -> p h j", p=P)
@@ -161,20 +161,26 @@ def tile_picked_fpn_none_e_kernel(
                 in_=result[:].rearrange("p i j -> p (i j)"),
             )
 
-        for first, count in ((PIECE, PIECE), (7 * part, part)):
-            nc.vector.tensor_copy(last[:, first : first + count], window(first, count))
-        for first, count in ((0, PIECE), (4 * part, part), (5 * part, part)):
-            nc.scalar.activation(last[:, first : first + count], window(first, count), COPY)
-        weave(nc.scalar.copy, PIECE, PIECE)
-        nc.scalar.activation(last[:, 6 * part : 7 * part], window(6 * part, part), COPY)
-        weave(nc.scalar.copy, 7 * part, part)
-        weave(nc.scalar.copy, 6 * part, part)
-        weave(nc.vector.tensor_copy, 0, PIECE)
-        weave(nc.vector.tensor_copy, 4 * part, part)
+        def scalar_gather(first):
+            nc.scalar.activation(last[:, first : first + part], window(first, part), COPY)
+
+        for first in (0, PIECE):
+            nc.vector.tensor_copy(last[:, first : first + part], window(first, part))
+        for first in (part, 3 * part, 5 * part, 4 * part, 6 * part):
+            scalar_gather(first)
+        weave(nc.scalar.copy, 5 * part, part)
+        scalar_gather(7 * part)
+        for first in (6 * part, 7 * part):
+            weave(nc.scalar.copy, first, part)
+        lap = 2
+        for first in (0, PIECE):
+            weave(nc.vector.tensor_copy, first + part + lap, part - lap)
+            weave(nc.vector.tensor_copy, first, part + lap)
         multiply(0, PIECE)
-        weave(nc.vector.tensor_copy, 5 * part, part)
+        weave(nc.vector.tensor_copy, 4 * part, part)
         multiply(PIECE, PIECE)
-        multiply(2 * PIECE, PIECE)
+        multiply(5 * part, part)
+        multiply(4 * part, part)
         add_and_store(0, 0)
         add_and_store(1, 0)
         add_and_store(0, 1)

@@ -161,26 +161,26 @@ def tile_picked_fpn_none_e_kernel(
                 in_=result[:].rearrange("p i j -> p (i j)"),
             )
 
-        def scalar_gather(first):
-            nc.scalar.activation(last[:, first : first + part], window(first, part), COPY)
+        def scalar_gather(first, count=part):
+            nc.scalar.activation(last[:, first : first + count], window(first, count), COPY)
 
-        for first in (0, PIECE):
+        for first in (0, HALF):
             nc.vector.tensor_copy(last[:, first : first + part], window(first, part))
-        for first in (part, 3 * part, 5 * part, 4 * part, 6 * part):
+        scalar_gather(part)
+        scalar_gather(PIECE, PIECE)
+        scalar_gather(5 * part)
+        for first in (4 * part, 5 * part):
+            weave(nc.scalar.copy, first, part)
+        for first in (6 * part, 7 * part):
             scalar_gather(first)
-        weave(nc.scalar.copy, 5 * part, part)
-        scalar_gather(7 * part)
         for first in (6 * part, 7 * part):
             weave(nc.scalar.copy, first, part)
         lap = 2
-        for first in (0, PIECE):
-            weave(nc.vector.tensor_copy, first + part + lap, part - lap)
-            weave(nc.vector.tensor_copy, first, part + lap)
-        multiply(0, PIECE)
-        weave(nc.vector.tensor_copy, 4 * part, part)
-        multiply(PIECE, PIECE)
-        multiply(5 * part, part)
-        multiply(4 * part, part)
+        weave(nc.vector.tensor_copy, part + lap, part - lap)
+        weave(nc.vector.tensor_copy, 0, part + lap)
+        weave(nc.vector.tensor_copy, PIECE, PIECE)
+        for first in range(0, 3 * PIECE, PIECE):
+            multiply(first, PIECE)
         add_and_store(0, 0)
         add_and_store(1, 0)
         add_and_store(0, 1)

@@ -179,7 +179,18 @@ def tile_picked_fpn_none_e_kernel(
         weave(nc.vector.tensor_copy, part + lap, part - lap)
         weave(nc.vector.tensor_copy, 0, part + lap)
         weave(nc.vector.tensor_copy, PIECE, PIECE)
-        for first in range(0, 3 * PIECE, PIECE):
+        codes0 = keep.tile([P, PIECE], U32, name="x0_codes", tag="x0_codes", align_bytes=64)
+        scales0 = keep.tile([P, PIECE], U8, name="x0_scales", align_bytes=64)
+        for first in (0, part):
+            half = slice(first, first + part)
+            nc.vector.quantize_mx(
+                out=codes0[:, half].bitcast(FP8X4),
+                scales=scales0[:, half],
+                in_=slot(first, part).rearrange("p c t -> p (c t)"),
+            )
+            product(accs[0, 0][:, half], w1_sb, w1_plane, 0, codes0[:, half], scales0[:, half])
+        product(accs[0, 1][:], w1_sb, w1_plane, 1, codes0, scales0)
+        for first in (PIECE, 2 * PIECE):
             multiply(first, PIECE)
         add_and_store(0, 0)
         add_and_store(1, 0)

@@ -21,6 +21,8 @@ PACK = 4
 HALF = S // 2
 PIECE = 256
 PIECES = S // PIECE
+PART = PIECE // 2
+LAP = 2
 
 
 def tile_picked_fpn_none_e_kernel(
@@ -53,7 +55,7 @@ def tile_picked_fpn_none_e_kernel(
         w2_sb = keep.tile([P, 2 * N], U8, name="w2_sb", align_bytes=64)
         w1_sb = keep.tile([P, 2 * N], U8, name="w1_sb", align_bytes=64)
         x_pair = keep.tile([P, 2, T], F32, name="x_pair")
-        x_rows = {t: keep.tile([P, T], F32, name=f"x_row{t}") for t in (2, 3)}
+        x_rows = {r: keep.tile([P, T], F32, name=f"x_row{r}") for r in (2, 3)}
         x_view = xT.rearrange("(p t) c -> p t c", t=PACK)
 
         nc.sync.dma_start(out=s_raw[:], in_=sT.rearrange("(p t) v -> p t v", t=PACK))
@@ -67,21 +69,21 @@ def tile_picked_fpn_none_e_kernel(
         nc.sync.dma_start(out=w1_sb[:].bitcast(I32), in_=w1_words[0].bitcast(I32))
         load_scales(w1_plane, w1_scales)
 
-        def quantize(name, grouped, width, pool=keep, tag=None):
-            codes = pool.tile([P, width], U32, name=name + "_codes", tag=tag or name + "_codes", align_bytes=64)
+        def mx_tiles(name, width, codes_tag=None):
+            codes = keep.tile([P, width], U32, name=name + "_codes", tag=codes_tag or name + "_codes", align_bytes=64)
             scales = keep.tile([P, width], U8, name=name + "_scales", align_bytes=64)
-            nc.vector.quantize_mx(
-                out=codes[:].bitcast(FP8X4), scales=scales[:], in_=grouped.rearrange("p c t -> p (c t)")
-            )
             return codes, scales
+
+        def quantize(codes, scales, values):
+            nc.vector.quantize_mx(out=codes.bitcast(FP8X4), scales=scales, in_=values.rearrange("p c t -> p (c t)"))
 
         def product(acc, w_sb, w_plane, h, codes, scales):
             nc.tensor.matmul_mx(
                 out=acc,
                 lhsT=w_sb[:, 2 * P * h : 2 * P * (h + 1)].bitcast(FP4X4),
                 lhsT_scale=w_plane[:, P * h : P * (h + 1)],
-                rhs=codes[:].bitcast(FP8X4),
-                rhs_scale=scales[:],
+                rhs=codes.bitcast(FP8X4),
+                rhs_scale=scales,
                 start=True,
                 stop=True,
             )
@@ -94,7 +96,9 @@ def tile_picked_fpn_none_e_kernel(
                 nc.vector.tensor_copy(out=s_grouped[:], in_=cells)
             else:
                 nc.scalar.copy(s_grouped[:], cells)
-            s_quantised.append(quantize(f"s{b}", s_grouped[:], V // 2))
+            codes, scales = mx_tiles(f"s{b}", V // 2)
+            quantize(codes[:], scales[:], s_grouped[:])
+            s_quantised.append((codes[:], scales[:]))
         t_sbs = []
         for h in range(N // P):
             t_acc = psum.tile([P, V], F32, name=f"t_acc{h}")
@@ -104,27 +108,24 @@ def tile_picked_fpn_none_e_kernel(
             nc.scalar.activation(t_sb[:], t_acc[:], COPY)
             t_sbs.append(t_sb)
 
-        parents = {}
-
-        def fetch_parents(piece):
-            parent = keep.tile([P, N // P, PIECE], F32, name=f"parent{piece}")
-            for h in range(N // P):
-                nc.vector.tensor_copy(parent[:, h, :], t_sbs[h][:].indirect(entries(par_sb, PIECE * piece, PIECE)))
-            parents[piece] = parent
-
         grouped = [keep.tile([P, HALF, PACK], BF16, name=f"grouped{b}", align_bytes=64) for b in range(2)]
 
         def slot(first, count):
             return grouped[first // HALF][:, first % HALF : first % HALF + count, :]
 
+        parents = []
         for piece in range(PIECES):
-            fetch_parents(piece)
+            parent = keep.tile([P, N // P, PIECE], F32, name=f"parent{piece}")
+            for h in range(N // P):
+                nc.vector.tensor_copy(parent[:, h, :], t_sbs[h][:].indirect(entries(par_sb, PIECE * piece, PIECE)))
+            parents.append(parent)
+
         picked01 = keep.tile([P, 2, HALF], F32, name="picked01")
-        for t in range(2):
-            nc.vector.tensor_copy(grouped[0][:, :, t], x_pair[:, t, :].indirect(entries(offs_sb, 0, HALF)))
-            nc.scalar.activation(picked01[:, t, :], x_pair[:, t, :].indirect(entries(offs_sb, HALF, HALF)), COPY)
+        for r in range(2):
+            nc.vector.tensor_copy(grouped[0][:, :, r], x_pair[:, r, :].indirect(entries(offs_sb, 0, HALF)))
+            nc.scalar.activation(picked01[:, r, :], x_pair[:, r, :].indirect(entries(offs_sb, HALF, HALF)), COPY)
         nc.scalar.copy(grouped[1][:, :, 0:2], picked01[:].rearrange("p t j -> p j t"))
-        part = PIECE // 2
+
         picked2 = keep.tile([P, S], BF16, name="picked2")
         for first in reversed(range(0, S, PIECE)):
             nc.vector.tensor_copy(picked2[:, first : first + PIECE], x_rows[2][:].indirect(entries(offs_sb, first, PIECE)))
@@ -137,6 +138,9 @@ def tile_picked_fpn_none_e_kernel(
         def window(first, count):
             return x_rows[3][:].indirect(entries(offs_sb, first, count))
 
+        def scalar_gather(first, count):
+            nc.scalar.activation(last[:, first : first + count], window(first, count), COPY)
+
         def weave(copy, first, count):
             copy(slot(first, count)[:, :, 3], last[:, first : first + count])
 
@@ -146,57 +150,48 @@ def tile_picked_fpn_none_e_kernel(
                 tag = f"t_acc{h}" if piece == PIECES - 1 else f"y_acc{piece}{h}"
                 accs[piece, h] = psum.tile([P, PIECE], F32, name=f"y_acc{piece}{h}", tag=tag)
 
-        def multiply(first, count, codes_tag=None):
-            quantised = quantize(f"x{first}", slot(first, count), count, keep, codes_tag)
-            at = first % PIECE
-            for h in range(N // P):
-                product(accs[first // PIECE, h][:, at : at + count], w1_sb, w1_plane, h, *quantised)
+        def row_halves(piece):
+            return (1, 0) if piece % 2 else (0, 1)
 
-        def add_and_store(h, *pieces):
-            result = keep.tile([P, len(pieces), PIECE], F32, name=f"result{pieces[0]}{h}")
-            for i, piece in enumerate(pieces):
-                nc.vector.tensor_tensor(result[:, i, :], accs[piece, h][:], parents[piece][:, h, :], ADD)
-            nc.sync.dma_start(
-                out=out_view[:, h, PIECE * pieces[0] : PIECE * (pieces[-1] + 1)],
-                in_=result[:].rearrange("p i j -> p (i j)"),
-            )
+        def multiply(piece, codes_tag=None):
+            codes, scales = mx_tiles(f"x{PIECE * piece}", PIECE, codes_tag)
+            quantize(codes[:], scales[:], slot(PIECE * piece, PIECE))
+            for h in row_halves(piece):
+                product(accs[piece, h][:], w1_sb, w1_plane, h, codes[:], scales[:])
 
-        def scalar_gather(first, count=part):
-            nc.scalar.activation(last[:, first : first + count], window(first, count), COPY)
+        def add_and_store(piece, h):
+            result = keep.tile([P, PIECE], F32, name=f"result{piece}{h}")
+            nc.vector.tensor_tensor(result[:], accs[piece, h][:], parents[piece][:, h, :], ADD)
+            nc.sync.dma_start(out=out_view[:, h, PIECE * piece : PIECE * (piece + 1)], in_=result[:])
 
-        for first in (0, HALF):
-            nc.vector.tensor_copy(last[:, first : first + part], window(first, part))
-        scalar_gather(part)
+        for first in (0, 2 * PIECE):
+            nc.vector.tensor_copy(last[:, first : first + PART], window(first, PART))
+        scalar_gather(PART, PART)
         scalar_gather(PIECE, PIECE)
-        scalar_gather(5 * part)
-        for first in (4 * part, 5 * part):
-            weave(nc.scalar.copy, first, part)
-        for first in (6 * part, 7 * part):
-            scalar_gather(first)
-        for first in (6 * part, 7 * part):
-            weave(nc.scalar.copy, first, part)
-        lap = 2
-        weave(nc.vector.tensor_copy, part + lap, part - lap)
-        weave(nc.vector.tensor_copy, 0, part + lap)
+        scalar_gather(2 * PIECE + PART, PART)
+        for first in (2 * PIECE, 2 * PIECE + PART):
+            weave(nc.scalar.copy, first, PART)
+        for first in (3 * PIECE, 3 * PIECE + PART):
+            scalar_gather(first, PART)
+        for first in (3 * PIECE, 3 * PIECE + PART):
+            weave(nc.scalar.copy, first, PART)
+        weave(nc.vector.tensor_copy, PART + LAP, PART - LAP)
+        weave(nc.vector.tensor_copy, 0, PART + LAP)
         weave(nc.vector.tensor_copy, PIECE, PIECE)
-        codes0 = keep.tile([P, PIECE], U32, name="x0_codes", tag="x0_codes", align_bytes=64)
-        scales0 = keep.tile([P, PIECE], U8, name="x0_scales", align_bytes=64)
-        for first in (0, part):
-            half = slice(first, first + part)
-            nc.vector.quantize_mx(
-                out=codes0[:, half].bitcast(FP8X4),
-                scales=scales0[:, half],
-                in_=slot(first, part).rearrange("p c t -> p (c t)"),
-            )
+
+        codes0, scales0 = mx_tiles("x0", PIECE)
+        for first in (0, PART):
+            half = slice(first, first + PART)
+            quantize(codes0[:, half], scales0[:, half], slot(first, PART))
             product(accs[0, 0][:, half], w1_sb, w1_plane, 0, codes0[:, half], scales0[:, half])
-        product(accs[0, 1][:], w1_sb, w1_plane, 1, codes0, scales0)
-        for first in (PIECE, 2 * PIECE):
-            multiply(first, PIECE)
+        product(accs[0, 1][:], w1_sb, w1_plane, 1, codes0[:], scales0[:])
+        multiply(1)
+        multiply(2)
         add_and_store(0, 0)
-        add_and_store(1, 0)
         add_and_store(0, 1)
-        multiply(6 * part, PIECE, "x0_codes")
         add_and_store(1, 1)
+        multiply(3, "x0_codes")
+        add_and_store(1, 0)
         for piece in (2, 3):
-            for h in range(N // P):
-                add_and_store(h, piece)
+            for h in row_halves(piece):
+                add_and_store(piece, h)

@@ -22,6 +22,7 @@ HALF = S // 2
 PIECE = 256
 PIECES = S // PIECE
 PART = PIECE // 2
+MORE = 32
 LAP = 2
 
 
@@ -164,10 +165,10 @@ def tile_picked_fpn_none_e_kernel(
             nc.vector.tensor_tensor(result[:], accs[piece, h][:], parents[piece][:, h, :], ADD)
             nc.sync.dma_start(out=out_view[:, h, PIECE * piece : PIECE * (piece + 1)], in_=result[:])
 
-        for first in (0, 2 * PIECE):
-            nc.vector.tensor_copy(last[:, first : first + PART], window(first, PART))
-        scalar_gather(PART, PART)
-        scalar_gather(PIECE, PIECE)
+        for first, count in ((PART, PART + MORE), (2 * PIECE, PART)):
+            nc.vector.tensor_copy(last[:, first : first + count], window(first, count))
+        scalar_gather(0, PART)
+        scalar_gather(PIECE + MORE, PIECE - MORE)
         scalar_gather(2 * PIECE + PART, PART)
         for first in (2 * PIECE, 2 * PIECE + PART):
             weave(nc.scalar.copy, first, PART)
@@ -175,9 +176,9 @@ def tile_picked_fpn_none_e_kernel(
             scalar_gather(first, PART)
         for first in (3 * PIECE, 3 * PIECE + PART):
             weave(nc.scalar.copy, first, PART)
-        weave(nc.vector.tensor_copy, PART + LAP, PART - LAP)
-        weave(nc.vector.tensor_copy, 0, PART + LAP)
-        weave(nc.vector.tensor_copy, PIECE, PIECE)
+        weave(nc.vector.tensor_copy, 0, PART - LAP)
+        weave(nc.vector.tensor_copy, PART - LAP, LAP + PART + MORE)
+        weave(nc.vector.tensor_copy, PIECE + MORE, PIECE - MORE)
 
         codes0, scales0 = mx_tiles("x0", PIECE)
         for first in (0, PART):

@@ -192,7 +192,5 @@ def tile_picked_fpn_none_e_kernel(
         add_and_store(0, 1)
         add_and_store(1, 1)
         multiply(3, "x0_codes")
-        add_and_store(1, 0)
-        for piece in (2, 3):
-            for h in row_halves(piece):
-                add_and_store(piece, h)
+        for piece, h in ((2, 0), (1, 0), (2, 1), (3, 1), (3, 0)):
+            add_and_store(piece, h)

@@ -22,8 +22,7 @@ HALF = S // 2
 PIECE = 256
 PIECES = S // PIECE
 PART = PIECE // 2
-MORE = 32
-LAP = 2
+LEAD = 160
 
 
 def tile_picked_fpn_none_e_kernel(
@@ -145,11 +144,12 @@ def tile_picked_fpn_none_e_kernel(
         def weave(copy, first, count):
             copy(slot(first, count)[:, :, 3], last[:, first : first + count])
 
-        accs = {}
+        accs = {(0, 0): [psum.tile([P, PART], F32, name=f"y_half{i}", tag=tag) for i, tag in enumerate(("t_acc0", "y_acc00"))]}
         for piece in range(PIECES):
             for h in range(N // P):
-                tag = f"t_acc{h}" if piece == PIECES - 1 else f"y_acc{piece}{h}"
-                accs[piece, h] = psum.tile([P, PIECE], F32, name=f"y_acc{piece}{h}", tag=tag)
+                if (piece, h) not in accs:
+                    tag = f"t_acc{h}" if piece == PIECES - 1 else f"y_acc{piece}{h}"
+                    accs[piece, h] = psum.tile([P, PIECE], F32, name=f"y_acc{piece}{h}", tag=tag)
 
         def row_halves(piece):
             return (1, 0) if piece % 2 else (0, 1)
@@ -165,10 +165,10 @@ def tile_picked_fpn_none_e_kernel(
             nc.vector.tensor_tensor(result[:], accs[piece, h][:], parents[piece][:, h, :], ADD)
             nc.sync.dma_start(out=out_view[:, h, PIECE * piece : PIECE * (piece + 1)], in_=result[:])
 
-        for first, count in ((PART, PART + MORE), (2 * PIECE, PART)):
+        for first, count in ((LEAD, HALF - 2 * LEAD), (2 * PIECE, PART)):
             nc.vector.tensor_copy(last[:, first : first + count], window(first, count))
-        scalar_gather(0, PART)
-        scalar_gather(PIECE + MORE, PIECE - MORE)
+        scalar_gather(0, LEAD)
+        scalar_gather(HALF - LEAD, LEAD)
         scalar_gather(2 * PIECE + PART, PART)
         for first in (2 * PIECE, 2 * PIECE + PART):
             weave(nc.scalar.copy, first, PART)
@@ -176,19 +176,22 @@ def tile_picked_fpn_none_e_kernel(
             scalar_gather(first, PART)
         for first in (3 * PIECE, 3 * PIECE + PART):
             weave(nc.scalar.copy, first, PART)
-        weave(nc.vector.tensor_copy, 0, PART - LAP)
-        weave(nc.vector.tensor_copy, PART - LAP, LAP + PART + MORE)
-        weave(nc.vector.tensor_copy, PIECE + MORE, PIECE - MORE)
+        weave(nc.vector.tensor_copy, 0, PART)
+        weave(nc.vector.tensor_copy, PART, HALF - LEAD - PART)
+        weave(nc.vector.tensor_copy, HALF - LEAD, LEAD)
 
         codes0, scales0 = mx_tiles("x0", PIECE)
-        for first in (0, PART):
-            half = slice(first, first + PART)
-            quantize(codes0[:, half], scales0[:, half], slot(first, PART))
-            product(accs[0, 0][:, half], w1_sb, w1_plane, 0, codes0[:, half], scales0[:, half])
+        halves = [slice(first, first + PART) for first in (0, PART)]
+        for half, acc in zip(halves, accs[0, 0]):
+            quantize(codes0[:, half], scales0[:, half], slot(half.start, PART))
+            product(acc[:], w1_sb, w1_plane, 0, codes0[:, half], scales0[:, half])
         product(accs[0, 1][:], w1_sb, w1_plane, 1, codes0[:], scales0[:])
         multiply(1)
         multiply(2)
-        add_and_store(0, 0)
+        result = keep.tile([P, PIECE], F32, name="result00")
+        for half, acc in zip(halves, accs[0, 0]):
+            nc.vector.tensor_tensor(result[:, half], acc[:], parents[0][:, 0, half], ADD)
+        nc.sync.dma_start(out=out_view[:, 0, 0:PIECE], in_=result[:])
         add_and_store(0, 1)
         add_and_store(1, 1)
         multiply(3, "x0_codes")

from contextlib import ExitStack

import concourse.mybir as mybir

K, T, S, V, N = 512, 4096, 1024, 512, 256
FLOPS = 2 * K * N * (S + V)

F32 = mybir.dt.float32
BF16 = mybir.dt.bfloat16
I32 = mybir.dt.int32
U32 = mybir.dt.uint32
U16 = mybir.dt.uint16
U8 = mybir.dt.uint8
FP8X4 = mybir.dt.float8_e4m3fn_x4
FP4X4 = mybir.dt.float4_e2m1fn_x4
ADD = mybir.AluOpType.add
COPY = mybir.ActivationFunctionType.Copy

P = 128
PACK = 4
HALF = S // 2
PIECE = 256
PIECES = S // PIECE
PART = PIECE // 2
LEAD = 160


def tile_picked_fpn_none_e_kernel(
    tc, xT, sT, w1_words, w1_scales, w2_words, w2_scales, offs, par, out
):
    nc = tc.nc
    with ExitStack() as ctx:
        keep = ctx.enter_context(tc.tile_pool(name="keep", bufs=1))
        psum = ctx.enter_context(tc.psum_pool(name="psum", bufs=1))

        offs_sb = keep.tile([P, S // 16], U16, name="offs_sb")
        par_sb = keep.tile([P, S // 16], U16, name="par_sb")

        def entries(list_sb, first, count):
            return list_sb[:, first // 16 : (first + count) // 16]

        w2_plane = keep.tile([P, N], U8, name="w2_plane", align_bytes=64)
        w1_plane = keep.tile([P, N], U8, name="w1_plane", align_bytes=64)
        for plane in (w2_plane, w1_plane):
            nc.vector.memset(plane[:].bitcast(I32), 0)

        def load_scales(plane, scales):
            for q in range(4):
                nc.sync.dma_start(
                    out=plane[32 * q : 32 * q + 4, :].bitcast(I32),
                    in_=scales[0, 4 * q : 4 * q + 4, :].bitcast(I32),
                )

        s_raw = keep.tile([P, PACK, V], F32, name="s_raw")
        w2_sb = keep.tile([P, 2 * N], U8, name="w2_sb", align_bytes=64)
        w1_sb = keep.tile([P, 2 * N], U8, name="w1_sb", align_bytes=64)
        x_pair = keep.tile([P, 2, T], F32, name="x_pair")
        x_rows = {r: keep.tile([P, T], F32, name=f"x_row{r}") for r in (2, 3)}
        x_view = xT.rearrange("(p t) c -> p t c", t=PACK)

        nc.sync.dma_start(out=s_raw[:], in_=sT.rearrange("(p t) v -> p t v", t=PACK))
        nc.sync.dma_start(out=w2_sb[:].bitcast(I32), in_=w2_words[0].bitcast(I32))
        nc.sync.dma_start(par_sb[:], par)
        load_scales(w2_plane, w2_scales)
        nc.sync.dma_start(out=x_pair[:], in_=x_view[:, 0:2, :])
        nc.sync.dma_start(offs_sb[:], offs)
        nc.sync.dma_start(out=x_rows[2][:], in_=x_view[:, 2, :])
        nc.sync.dma_start(out=x_rows[3][:], in_=x_view[:, 3, :])
        nc.sync.dma_start(out=w1_sb[:].bitcast(I32), in_=w1_words[0].bitcast(I32))
        load_scales(w1_plane, w1_scales)

        def mx_tiles(name, width, codes_tag=None):
            codes = keep.tile([P, width], U32, name=name + "_codes", tag=codes_tag or name + "_codes", align_bytes=64)
            scales = keep.tile([P, width], U8, name=name + "_scales", align_bytes=64)
            return codes, scales

        def quantize(codes, scales, values):
            nc.vector.quantize_mx(out=codes.bitcast(FP8X4), scales=scales, in_=values.rearrange("p c t -> p (c t)"))

        def product(acc, w_sb, w_plane, h, codes, scales):
            nc.tensor.matmul_mx(
                out=acc,
                lhsT=w_sb[:, 2 * P * h : 2 * P * (h + 1)].bitcast(FP4X4),
                lhsT_scale=w_plane[:, P * h : P * (h + 1)],
                rhs=codes.bitcast(FP8X4),
                rhs_scale=scales,
                start=True,
                stop=True,
            )

        s_quantised = []
        for b in range(2):
            cells = s_raw[:, :, V // 2 * b : V // 2 * (b + 1)].rearrange("p t v -> p v t")
            s_grouped = keep.tile([P, V // 2, PACK], BF16, name=f"s_grouped{b}", align_bytes=64)
            if b == 0:
                nc.vector.tensor_copy(out=s_grouped[:], in_=cells)
            else:
                nc.scalar.copy(s_grouped[:], cells)
            codes, scales = mx_tiles(f"s{b}", V // 2)
            quantize(codes[:], scales[:], s_grouped[:])
            s_quantised.append((codes[:], scales[:]))
        t_sbs = []
        for h in range(N // P):
            t_acc = psum.tile([P, V], F32, name=f"t_acc{h}")
            for b in range(2):
                product(t_acc[:, V // 2 * b : V // 2 * (b + 1)], w2_sb, w2_plane, h, *s_quantised[b])
            t_sb = keep.tile([P, V], F32, name=f"t_sb{h}")
            nc.scalar.activation(t_sb[:], t_acc[:], COPY)
            t_sbs.append(t_sb)

        grouped = [keep.tile([P, HALF, PACK], BF16, name=f"grouped{b}", align_bytes=64) for b in range(2)]

        def slot(first, count):
            return grouped[first // HALF][:, first % HALF : first % HALF + count, :]

        parents = []
        for piece in range(PIECES):
            parent = keep.tile([P, N // P, PIECE], F32, name=f"parent{piece}")
            for h in range(N // P):
                nc.vector.tensor_copy(parent[:, h, :], t_sbs[h][:].indirect(entries(par_sb, PIECE * piece, PIECE)))
            parents.append(parent)

        picked01 = keep.tile([P, 2, HALF], F32, name="picked01")
        for r in range(2):
            nc.vector.tensor_copy(grouped[0][:, :, r], x_pair[:, r, :].indirect(entries(offs_sb, 0, HALF)))
            nc.scalar.activation(picked01[:, r, :], x_pair[:, r, :].indirect(entries(offs_sb, HALF, HALF)), COPY)
        nc.scalar.copy(grouped[1][:, :, 0:2], picked01[:].rearrange("p t j -> p j t"))

        picked2 = keep.tile([P, S], BF16, name="picked2")
        for first in reversed(range(0, S, PIECE)):
            nc.vector.tensor_copy(picked2[:, first : first + PIECE], x_rows[2][:].indirect(entries(offs_sb, first, PIECE)))
            copy = nc.scalar.copy if first > 0 else nc.vector.tensor_copy
            copy(slot(first, PIECE)[:, :, 2], picked2[:, first : first + PIECE])

        out_view = out.rearrange("(h p) j -> p h j", p=P)
        last = keep.tile([P, S], BF16, name="last")

        def window(first, count):
            return x_rows[3][:].indirect(entries(offs_sb, first, count))

        def scalar_gather(first, count):
            nc.scalar.activation(last[:, first : first + count], window(first, count), COPY)

        def weave(copy, first, count):
            copy(slot(first, count)[:, :, 3], last[:, first : first + count])

        accs = {(0, 0): [psum.tile([P, PART], F32, name=f"y_half{i}", tag=tag) for i, tag in enumerate(("t_acc0", "y_acc00"))]}
        for piece in range(PIECES):
            for h in range(N // P):
                if (piece, h) not in accs:
                    tag = f"t_acc{h}" if piece == PIECES - 1 else f"y_acc{piece}{h}"
                    accs[piece, h] = psum.tile([P, PIECE], F32, name=f"y_acc{piece}{h}", tag=tag)

        def row_halves(piece):
            return (1, 0) if piece % 2 else (0, 1)

        def multiply(piece, codes_tag=None):
            codes, scales = mx_tiles(f"x{PIECE * piece}", PIECE, codes_tag)
            quantize(codes[:], scales[:], slot(PIECE * piece, PIECE))
            for h in row_halves(piece):
                product(accs[piece, h][:], w1_sb, w1_plane, h, codes[:], scales[:])

        def add_and_store(piece, h):
            result = keep.tile([P, PIECE], F32, name=f"result{piece}{h}")
            nc.vector.tensor_tensor(result[:], accs[piece, h][:], parents[piece][:, h, :], ADD)
            nc.sync.dma_start(out=out_view[:, h, PIECE * piece : PIECE * (piece + 1)], in_=result[:])

        for first, count in ((LEAD, HALF - 2 * LEAD), (2 * PIECE, PART)):
            nc.vector.tensor_copy(last[:, first : first + count], window(first, count))
        scalar_gather(0, LEAD)
        scalar_gather(HALF - LEAD, LEAD)
        scalar_gather(2 * PIECE + PART, PART)
        for first in (2 * PIECE, 2 * PIECE + PART):
            weave(nc.scalar.copy, first, PART)
        for first in (3 * PIECE, 3 * PIECE + PART):
            scalar_gather(first, PART)
        for first in (3 * PIECE, 3 * PIECE + PART):
            weave(nc.scalar.copy, first, PART)
        weave(nc.vector.tensor_copy, 0, PART)
        weave(nc.vector.tensor_copy, PART, HALF - LEAD - PART)
        weave(nc.vector.tensor_copy, HALF - LEAD, LEAD)

        codes0, scales0 = mx_tiles("x0", PIECE)
        halves = [slice(first, first + PART) for first in (0, PART)]
        for half, acc in zip(halves, accs[0, 0]):
            quantize(codes0[:, half], scales0[:, half], slot(half.start, PART))
            product(acc[:], w1_sb, w1_plane, 0, codes0[:, half], scales0[:, half])
        product(accs[0, 1][:], w1_sb, w1_plane, 1, codes0[:], scales0[:])
        multiply(1)
        multiply(2)
        result = keep.tile([P, PIECE], F32, name="result00")
        for half, acc in zip(halves, accs[0, 0]):
            nc.vector.tensor_tensor(result[:, half], acc[:], parents[0][:, 0, half], ADD)
        nc.sync.dma_start(out=out_view[:, 0, 0:PIECE], in_=result[:])
        add_and_store(0, 1)
        add_and_store(1, 1)
        multiply(3, "x0_codes")
        for piece, h in ((2, 0), (1, 0), (2, 1), (3, 1), (3, 0)):
            add_and_store(piece, h)
